import numpy as np
import ml_dtypes


def mxq(x, axis, fmt="e4m3"):
    dtype, down = {"e4m3": (ml_dtypes.float8_e4m3fn, 7), "e5m2": (ml_dtypes.float8_e5m2, 14)}[fmt]
    v = np.moveaxis(np.asarray(x, np.float32).astype(ml_dtypes.bfloat16).astype(np.float64), axis, -1)
    blocks = v.reshape(v.shape[:-1] + (-1, 32))
    amax = np.abs(blocks).max(-1, keepdims=True)
    byte = np.maximum(np.where(amax > 0, np.frexp(amax)[1] - 1 + 127, 0) - down, 1)
    scale = np.exp2(byte - 127.0)
    codes = (blocks / scale).astype(np.float32).astype(dtype).astype(np.float64)
    return np.moveaxis((codes * scale).reshape(v.shape), -1, axis)


WIDE = False


def mx_kscale(k):
    if not WIDE:
        return np.ones(k)
    levels = np.array([10, -10, 5, -5, 0])
    if k % 512:
        return np.exp2(np.random.permutation(np.resize(levels, k // 32))).repeat(32)
    a = np.empty((k // 512, 16))
    for p in range(k // 512):
        a[p, :8] = np.random.permutation(np.resize(levels, 8))
        for g in range(8):
            far = levels[np.abs(levels - a[p, g]) >= 10]
            a[p, g + 8] = far[np.random.randint(len(far))]
    return np.exp2(a.ravel()).repeat(32)


def f64(x):
    return np.asarray(x).astype(np.float64)


def striped(idx):
    return np.tile(np.asarray(idx).reshape(-1, 16).T, (8, 1)).astype(np.uint16)


def unstriped(offs):
    return offs[:16].T.reshape(-1).astype(np.int64)


def striped8(idx):
    return np.asarray(idx).reshape(8, -1, 16).transpose(0, 2, 1).reshape(128, -1).astype(np.uint16)


def unstriped8(offs):
    return offs.reshape(8, 16, -1).transpose(0, 2, 1).reshape(8, -1).astype(np.int64)


def pick8(x, idx, run):
    r = np.arange(len(x))
    return x[r[:, None], idx[r % (8 * run) // run]]


E2M1 = np.array([0.0, 0.5, 1.0, 1.5, 2.0, 3.0, 4.0, 6.0, -0.0, -0.5, -1.0, -1.5, -2.0, -3.0, -4.0, -6.0])


def pack_weight(w, fmt):
    k, n = w.shape
    w = f64(np.asarray(w, np.float32).astype(ml_dtypes.bfloat16)).reshape(k // 32, 32, n)
    amax = np.abs(w).max(1)
    if fmt == "e4m3":
        byte = np.frexp(amax)[1] - 1 + 127 - 7
    else:
        mant, ex = np.frexp(amax / 6.0)
        byte = np.where(mant > 0.5, ex, ex - 1) + 127
    byte = np.clip(np.where(amax > 0, byte, 1), 1, 254)
    scaled = (w * np.exp2(127.0 - byte)[:, None, :]).reshape(k, n).astype(np.float32)
    by_word = np.ascontiguousarray(scaled.reshape(k // 512, 128, 4, n).transpose(0, 1, 3, 2))
    if fmt == "e4m3":
        words = by_word.astype(ml_dtypes.float8_e4m3fn).view(np.uint8)
    else:
        c = by_word.astype(ml_dtypes.float4_e2m1fn).view(np.uint8) & 0xF
        words = (c[..., 0::2] | (c[..., 1::2] << 4)).reshape(k // 512, 128, 2 * n)
    return np.ascontiguousarray(words), np.ascontiguousarray(byte.astype(np.uint8).reshape(k // 512, 16, n))


def unpack_weight(words, scales, fmt):
    g, _, n = scales.shape
    words = np.ascontiguousarray(words).reshape(g, 128, n, -1)
    if fmt == "e4m3":
        vals = words.view(ml_dtypes.float8_e4m3fn).astype(np.float64)
    else:
        nib = np.empty((g, 128, n, 4), np.uint8)
        nib[..., 0::2] = words & 0xF
        nib[..., 1::2] = words >> 4
        vals = E2M1[nib]
    vals = vals * np.repeat(np.exp2(scales.astype(np.float64) - 127.0), 8, axis=1)[..., None]
    return vals.transpose(0, 1, 3, 2).reshape(g * 512, n)


def sigmoid(v):
    return 1.0 / (1.0 + np.exp(-v))


def bf(x):
    return np.asarray(x, np.float32).astype(ml_dtypes.bfloat16)


def planes(Y):
    r, m = Y.shape
    b = f64(bf(Y)).reshape(r // 32, 32, m)
    amax = np.abs(b).max(1)
    byte = np.clip(np.where(amax > 0, np.frexp(amax)[1] - 1 + 127 - 7, 1), 1, 254)
    codes = (b * np.exp2(127.0 - byte)[:, None, :]).reshape(r, m).astype(np.float32).astype(ml_dtypes.float8_e4m3fn).view(np.uint8)
    words = codes.reshape(r // 512, 128, 4, m).transpose(0, 1, 3, 2)
    return np.ascontiguousarray(words), np.ascontiguousarray(byte.astype(np.uint8).reshape(r // 512, 16, m))


K, R, F, T, J, M = 512, 512, 512, 2048, 512, 256


def setup_inputs():
    n = np.random.standard_normal
    idx = np.random.permutation(T)[:J]
    idx2 = np.stack([np.random.permutation(J)[:M] for _ in range(8)])
    fk = mx_kscale(K)
    ff = mx_kscale(F)
    tabp = pack_weight(n((K, T)) / fk[:, None], "e4m3")
    return {
        "tab_words": tabp[0],
        "tab_scales": tabp[1],
        "w1": (n((K, R)) * 1 / np.sqrt(K) * fk[:, None]).astype(np.float32),
        "bias": (np.random.uniform(-0.5, 0.5, (R, 1))).astype(np.float32),
        "gain": (np.random.uniform(0.5, 1.5, (R, 1))).astype(np.float32),
        "pw": (np.random.uniform(0.5, 1.5, (1, M))).astype(np.float32),
        "wo": (n((F, R)) * 1 / np.sqrt(F) * ff[:, None]).astype(np.float32),
        "dy": (n((F, M)) / ff[:, None]).astype(np.float32),
        "old": (0.5 * n((R, J))).astype(np.float32),
        "offs": striped(idx),
        "offs2": striped8(idx2),
    }


def reference(tab_words, tab_scales, w1, bias, gain, pw, wo, dy, old, offs, offs2):
    idx = unstriped(offs)
    idx2 = unstriped8(offs2)
    tabu = unpack_weight(tab_words, tab_scales, "e4m3")
    w1q = mxq(f64(w1), 0, "e4m3")
    tabidxg = tabu[:, idx]
    a = w1q.T @ tabidxg
    h1 = np.tanh(a + f64(bias))
    h2 = h1 * f64(gain)
    s = pick8(h2, idx2, 64) * f64(pw)
    woq = mxq(f64(wo), 0, "e4m3")
    dyq = mxq(f64(dy), 0, "e4m3")
    c0 = woq.T @ dyq
    ds = c0 * sigmoid(s) * (1.0 + s * (1.0 - sigmoid(s)))
    e1 = ds * f64(pw)
    s1 = np.zeros((R, J))
    s1[np.arange(R)[:, None], idx2[np.arange(R) % 512 // 64]] = e1
    dh1 = s1 * f64(gain)
    da = dh1 * (1.0 - np.square(h1))
    y = da + f64(old)
    words, scales = planes(y)
    return y, words, scales

@@ -1,0 +1,232 @@
+from contextlib import ExitStack
+
+import concourse.mybir as mybir
+from concourse.masks import make_identity
+
+K, R, F, T, J, M = 512, 512, 512, 2048, 512, 256
+FLOPS = 2 * K * R * J + 2 * F * R * M
+
+F32 = mybir.dt.float32
+BF16 = mybir.dt.bfloat16
+I32 = mybir.dt.int32
+U32 = mybir.dt.uint32
+U16 = mybir.dt.uint16
+U8 = mybir.dt.uint8
+FP8X4 = mybir.dt.float8_e4m3fn_x4
+ACT = mybir.ActivationFunctionType
+ALU = mybir.AluOpType
+
+P = 128
+PACK = 4
+
+
+def tile_attend_cpickact_pl_kernel(tc, tab_words, tab_scales, w1, bias, gain, pw, wo, dy, old, offs, offs2, out_0, out_1, out_2):
+    nc = tc.nc
+    with ExitStack() as ctx:
+        sb = ctx.enter_context(tc.tile_pool(name="sb", bufs=1))
+        ps = ctx.enter_context(tc.psum_pool(name="ps", bufs=1))
+
+        def sbt(name, shape, dtype, tag=None):
+            return sb.tile(shape, dtype, name=name, tag=tag or name, align_bytes=64)
+
+        slot_list = sbt("slot_list", [P, J // 16], U16)
+        pick_lists = sbt("pick_lists", [P, M // 16], U16)
+        tabw = sbt("tabw", [P, T], U32, "tabw_old")
+        tabs = sbt("tabs", [P, T], U8, "tabs_dy")
+        w1_raw = sbt("w1_raw", [P, PACK, R], F32, "w_raw")
+        bias_sb = sbt("bias_sb", [P, PACK], F32)
+        gain_sb = sbt("gain_sb", [P, PACK], F32)
+        pw_cols = sbt("pw_cols", [P, 2], F32)
+        s1 = [sbt("s1_%d" % t, [P, J], F32) for t in range(PACK)]
+
+        nc.vector.memset(tabs[:].bitcast(I32), 0)
+        nc.sync.dma_start(slot_list[:], offs)
+        nc.sync.dma_start(w1_raw[:], w1.rearrange("(p j) r -> p j r", j=PACK))
+        for q in range(4):
+            nc.scalar.dma_start(tabs[32 * q : 32 * q + 4, :].bitcast(I32), tab_scales[0, 4 * q : 4 * q + 4, :].bitcast(I32))
+        nc.sync.dma_start(tabw[:].bitcast(I32), tab_words[0].rearrange("p n t -> p (n t)").bitcast(I32))
+        nc.sync.dma_start(pick_lists[:], offs2)
+        nc.gpsimd.dma_start(bias_sb[:], bias.rearrange("(p t) o -> p (t o)", t=PACK))
+        nc.gpsimd.dma_start(gain_sb[:], gain.rearrange("(p t) o -> p (t o)", t=PACK))
+        nc.gpsimd.dma_start(pw_cols[:], pw.rearrange("o (p h) -> p (o h)", h=2))
+        ident = sbt("ident", [P, P], F32)
+        make_identity(nc, ident[:])
+        for t in range(PACK):
+            nc.vector.memset(s1[t][:], 0.0)
+
+        warm = sbt("warm", [P, 8], F32)
+        nc.scalar.activation(warm[:], s1[0][:, 0:8], ACT.Silu)
+
+        pw_bank = ps.tile([P, 2, P], F32, name="pw_bank", tag="c0t0")
+        for h in range(2):
+            nc.tensor.transpose(pw_bank[:, h, :], pw_cols[:, h : h + 1].to_broadcast([P, P]), ident[:])
+        pw_row = sbt("pw_row", [P, M], F32)
+        nc.scalar.copy(pw_row[:].rearrange("q (p h) -> q p h", h=2), pw_bank[:].rearrange("q h p -> q p h"))
+        neg_gain = sbt("neg_gain", [P, PACK], F32)
+        nc.scalar.activation(neg_gain[:], gain_sb[:], ACT.Copy, scale=-1.0)
+
+        gs = sbt("gs", [P, J], U8)
+        nc.vector.tensor_copy(gs[:], tabs[:].indirect(slot_list[:]))
+        dy_raw = sbt("dy_raw", [P, PACK, M], F32, "tabs_dy")
+        nc.sync.dma_start(dy_raw[:], dy.rearrange("(p j) m -> p j m", j=PACK))
+        w1_bf = sbt("w1_bf", [P, PACK * R], BF16)
+        nc.vector.tensor_copy(
+            w1_bf[:].rearrange("p (t m j) -> p m j t", t=PACK, j=PACK),
+            w1_raw[:].rearrange("p j (m t) -> p m j t", t=PACK),
+        )
+        wo_raw = sbt("wo_raw", [P, PACK, R], F32, "w_raw")
+        nc.sync.dma_start(wo_raw[:], wo.rearrange("(p j) r -> p j r", j=PACK))
+        w1_codes = sbt("w1_codes", [P, R], U32)
+        w1_scales = sbt("w1_scales", [P, R], U8)
+        nc.vector.quantize_mx(out=w1_codes[:].bitcast(FP8X4), scales=w1_scales[:], in_=w1_bf[:])
+        gw = sbt("gw", [P, J], U32)
+        nc.vector.tensor_copy(gw[:], tabw[:].indirect(slot_list[:]))
+        old_sb = sbt("old_sb", [P, PACK, J], F32, "tabw_old")
+        nc.sync.dma_start(old_sb[:], old.rearrange("(p t) j -> p t j", t=PACK))
+
+        a_banks = [ps.tile([P, J], F32, name="a%d" % t) for t in range(PACK)]
+        for t in range(PACK):
+            cols = slice(t * P, (t + 1) * P)
+            nc.tensor.matmul_mx(
+                out=a_banks[t][:], lhsT=w1_codes[:, cols].bitcast(FP8X4), lhsT_scale=w1_scales[:, cols],
+                rhs=gw[:].bitcast(FP8X4), rhs_scale=gs[:], start=True, stop=True,
+            )
+
+        dy_bf = sbt("dy_bf", [P, PACK * M], BF16)
+        nc.vector.tensor_copy(
+            dy_bf[:].rearrange("p (h n j) -> p n j h", h=2, j=PACK),
+            dy_raw[:].rearrange("p j (n h) -> p n j h", h=2),
+        )
+        dy_codes = sbt("dy_codes", [P, M], U32)
+        dy_scales = sbt("dy_scales", [P, M], U8)
+        nc.vector.quantize_mx(out=dy_codes[:].bitcast(FP8X4), scales=dy_scales[:], in_=dy_bf[:])
+
+        h1 = [sbt("h1_%d" % t, [P, J], F32) for t in range(PACK)]
+        h2 = [sbt("h2_%d" % t, [P, J], F32) for t in range(PACK)]
+        sq = [sbt("sq_%d" % t, [P, J], F32) for t in range(PACK)]
+        s = [sbt("s_%d" % t, [P, M], F32) for t in range(PACK)]
+        nsil = [sbt("nsil_%d" % t, [P, M], F32) for t in range(PACK)]
+        th = [sbt("th_%d" % t, [P, M], F32) for t in range(PACK)]
+        nsig = [sbt("nsig_%d" % t, [P, M], F32) for t in range(PACK)]
+        part = [sbt("part_%d" % t, [P, M], F32) for t in range(PACK)]
+        nda = [sbt("nda_%d" % t, [P, J], F32) for t in range(PACK)]
+        y = sbt("y", [P, PACK, J], F32)
+
+        def forward(t):
+            nc.scalar.activation(h1[t][:], a_banks[t][:], ACT.Tanh, bias=bias_sb[:, t : t + 1])
+            nc.scalar.activation(h2[t][:], h1[t][:], ACT.Copy, scale=gain_sb[:, t : t + 1])
+
+        def pick(t):
+            nc.vector.tensor_tensor(s[t][:], h2[t][:].indirect(pick_lists[:]), pw_row[:], ALU.mult)
+
+        def silu_parts(t):
+            nc.scalar.activation(nsil[t][:], s[t][:], ACT.Silu, scale=-1.0)
+            nc.scalar.activation(th[t][:], s[t][:], ACT.Tanh, scale=0.5)
+            nc.scalar.activation(nsig[t][:], th[t][:], ACT.Copy, scale=-0.5, bias=-0.5)
+
+        forward(0)
+        pick(0)
+        forward(1)
+
+        wo_bf = sbt("wo_bf", [P, PACK * R], BF16)
+        nc.vector.tensor_copy(
+            wo_bf[:].rearrange("p (c i j) -> p c j i", i=4, j=PACK),
+            wo_raw[:].rearrange("p j (c i) -> p c j i", i=4),
+        )
+        pick(1)
+        wo_codes = sbt("wo_codes", [P, R], U32)
+        wo_scales = sbt("wo_scales", [P, R], U8)
+        nc.vector.quantize_mx(out=wo_codes[:].bitcast(FP8X4), scales=wo_scales[:], in_=wo_bf[:])
+        forward(2)
+        forward(3)
+        c0t_banks = [ps.tile([P, R], F32, name="c0t_bank%d" % h, tag="c0t%d" % h) for h in range(2)]
+        cpt = [sbt("cpt_%d" % h, [P, PACK, P], F32) for h in range(2)]
+        for h in range(2):
+            cols = slice(h * P, (h + 1) * P)
+            nc.tensor.matmul_mx(
+                out=c0t_banks[h][:], lhsT=dy_codes[:, cols].bitcast(FP8X4), lhsT_scale=dy_scales[:, cols],
+                rhs=wo_codes[:].bitcast(FP8X4), rhs_scale=wo_scales[:], start=True, stop=True,
+            )
+        pick(2)
+        silu_parts(0)
+        for h in range(2):
+            nc.scalar.activation(
+                cpt[h][:], c0t_banks[h][:].rearrange("m (p t) -> m t p", t=PACK), ACT.Copy, scale=pw_cols[:, h : h + 1]
+            )
+        cp_banks = [ps.tile([P, 2, 2, P], F32, name="cp_bank%d" % u) for u in range(2)]
+        for t in range(PACK):
+            for h in range(2):
+                nc.tensor.transpose(cp_banks[t // 2][:, t % 2, h, :], cpt[h][:, t, :], ident[:])
+        pick(3)
+        silu_parts(1)
+        nc.scalar.activation(sq[0][:], h1[0][:], ACT.Square)
+        silu_parts(2)
+        nc.scalar.activation(sq[1][:], h1[1][:], ACT.Square)
+        silu_parts(3)
+        nc.scalar.activation(sq[2][:], h1[2][:], ACT.Square)
+        nc.scalar.activation(sq[3][:], h1[3][:], ACT.Square)
+
+        def grad_part(t):
+            nc.vector.scalar_tensor_tensor(
+                part[t][:].rearrange("r (n h) -> r n h", h=2),
+                nsil[t][:].rearrange("r (n h) -> r n h", h=2),
+                1.0,
+                cp_banks[t // 2][:, t % 2, :, :].rearrange("r h n -> r n h"),
+                ALU.subtract, ALU.mult,
+            )
+
+        def scatter(t):
+            nc.vector.tensor_tensor(s1[t][:].indirect(pick_lists[:]), part[t][:], nsig[t][:], ALU.mult)
+
+        def tanh_grad(t, cols):
+            nc.vector.scalar_tensor_tensor(nda[t][:, cols], sq[t][:, cols], 1.0, s1[t][:, cols], ALU.subtract, ALU.mult)
+
+        out_rows = out_0.rearrange("(p t) j -> p t j", t=PACK)
+
+        def add_old(t, cols):
+            nc.vector.scalar_tensor_tensor(
+                y[:, t, cols], nda[t][:, cols], neg_gain[:, t : t + 1], old_sb[:, t, cols], ALU.mult, ALU.add
+            )
+
+        whole = slice(0, J)
+        grad_part(0)
+        grad_part(1)
+        scatter(0)
+        scatter(1)
+        tanh_grad(0, whole)
+        grad_part(2)
+        add_old(0, whole)
+        nc.sync.dma_start(out_rows[:, 0, :], y[:, 0, :])
+        tanh_grad(1, whole)
+        scatter(2)
+        add_old(1, whole)
+        nc.sync.dma_start(out_rows[:, 1, :], y[:, 1, :])
+        grad_part(3)
+        tanh_grad(2, whole)
+        scatter(3)
+        add_old(2, whole)
+        nc.sync.dma_start(out_rows[:, 2, :], y[:, 2, :])
+        halves = [slice(0, J // 2), slice(J // 2, J)]
+        tanh_grad(3, halves[0])
+        tanh_grad(3, halves[1])
+        add_old(3, halves[0])
+        add_old(3, halves[1])
+        nc.sync.dma_start(out_rows[:, 3, :], y[:, 3, :])
+
+        y_bf = [sbt("y_bf%d" % u, [P, PACK * J // 2], BF16) for u in range(2)]
+        y_codes = sbt("y_codes", [P, J], U32)
+        y_scales = sbt("y_scales", [P, J], U8)
+        nc.scalar.copy(
+            y_bf[0][:].rearrange("p (c i t) -> p c t i", i=4, t=PACK),
+            y[:, :, halves[0]].rearrange("p t (c i) -> p c t i", i=4),
+        )
+        nc.vector.tensor_copy(
+            y_bf[1][:].rearrange("p (c i t) -> p c t i", i=4, t=PACK),
+            y[:, :, halves[1]].rearrange("p t (c i) -> p c t i", i=4),
+        )
+        words_out = out_1[0].rearrange("p n t -> p (n t)").bitcast(I32)
+        for u in (1, 0):
+            nc.vector.quantize_mx(out=y_codes[:, halves[u]].bitcast(FP8X4), scales=y_scales[:, halves[u]], in_=y_bf[u][:])
+            nc.sync.dma_start(words_out[:, halves[u]], y_codes[:, halves[u]].bitcast(I32))
+        for q in range(4):
+            nc.scalar.dma_start(out_2[0, 4 * q : 4 * q + 4, :].bitcast(I32), y_scales[32 * q : 32 * q + 4, :].bitcast(I32))

@@ -31,24 +31,33 @@ def tile_attend_cpickact_pl_kernel(tc, tab_words, tab_scales, w1, bias, gain, pw
 
         slot_list = sbt("slot_list", [P, J // 16], U16)
         pick_lists = sbt("pick_lists", [P, M // 16], U16)
-        tabw = sbt("tabw", [P, T], U32, "tabw_old")
-        tabs = sbt("tabs", [P, T], U8, "tabs_dy")
-        w1_raw = sbt("w1_raw", [P, PACK, R], F32, "w_raw")
+        tabw = sbt("tabw", [P, T], U32)
+        tabs = sbt("tabs", [P, T], U8)
+        w1_raw = sbt("w1_raw", [P, PACK, R], F32)
+        wo_raw = [sbt("wo_raw%d" % u, [P, PACK, R // 2], F32) for u in range(2)]
+        tabs_in = sbt("tabs_in", [P, T // 4], I32)
+        dy_raw = sbt("dy_raw", [P, PACK, M], F32)
+        old_sb = sbt("old_sb", [P, PACK, J], F32)
         bias_sb = sbt("bias_sb", [P, PACK], F32)
         gain_sb = sbt("gain_sb", [P, PACK], F32)
         pw_cols = sbt("pw_cols", [P, 2], F32)
         s1 = [sbt("s1_%d" % t, [P, J], F32) for t in range(PACK)]
 
+        for q in range(4):
+            queue = nc.sync if q % 2 == 0 else nc.scalar
+            queue.dma_start(tabs_in[32 * q : 32 * q + 4, :], tab_scales[0, 4 * q : 4 * q + 4, :].bitcast(I32))
         nc.vector.memset(tabs[:].bitcast(I32), 0)
         nc.sync.dma_start(slot_list[:], offs)
+        nc.scalar.dma_start(pw_cols[:], pw.rearrange("o (p h) -> p (o h)", h=2))
         nc.sync.dma_start(w1_raw[:], w1.rearrange("(p j) r -> p j r", j=PACK))
-        for q in range(4):
-            nc.scalar.dma_start(tabs[32 * q : 32 * q + 4, :].bitcast(I32), tab_scales[0, 4 * q : 4 * q + 4, :].bitcast(I32))
         nc.sync.dma_start(tabw[:].bitcast(I32), tab_words[0].rearrange("p n t -> p (n t)").bitcast(I32))
+        nc.sync.dma_start(bias_sb[:], bias.rearrange("(p t) o -> p (t o)", t=PACK))
+        nc.sync.dma_start(gain_sb[:], gain.rearrange("(p t) o -> p (t o)", t=PACK))
         nc.sync.dma_start(pick_lists[:], offs2)
-        nc.gpsimd.dma_start(bias_sb[:], bias.rearrange("(p t) o -> p (t o)", t=PACK))
-        nc.gpsimd.dma_start(gain_sb[:], gain.rearrange("(p t) o -> p (t o)", t=PACK))
-        nc.gpsimd.dma_start(pw_cols[:], pw.rearrange("o (p h) -> p (o h)", h=2))
+        nc.sync.dma_start(dy_raw[:], dy.rearrange("(p j) m -> p j m", j=PACK))
+        for u in range(2):
+            nc.sync.dma_start(wo_raw[u][:], wo.rearrange("(p j) r -> p j r", j=PACK)[:, :, u * R // 2 : (u + 1) * R // 2])
+        nc.sync.dma_start(old_sb[:], old.rearrange("(p t) j -> p t j", t=PACK))
         ident = sbt("ident", [P, P], F32)
         make_identity(nc, ident[:])
         for t in range(PACK):
@@ -65,32 +74,33 @@ def tile_attend_cpickact_pl_kernel(tc, tab_words, tab_scales, w1, bias, gain, pw
         neg_gain = sbt("neg_gain", [P, PACK], F32)
         nc.scalar.activation(neg_gain[:], gain_sb[:], ACT.Copy, scale=-1.0)
 
+        for q in range(4):
+            nc.vector.tensor_copy(tabs[32 * q : 32 * q + 4, :].bitcast(I32), tabs_in[32 * q : 32 * q + 4, :])
         gs = sbt("gs", [P, J], U8)
         nc.vector.tensor_copy(gs[:], tabs[:].indirect(slot_list[:]))
-        dy_raw = sbt("dy_raw", [P, PACK, M], F32, "tabs_dy")
-        nc.sync.dma_start(dy_raw[:], dy.rearrange("(p j) m -> p j m", j=PACK))
-        w1_bf = sbt("w1_bf", [P, PACK * R], BF16)
-        nc.vector.tensor_copy(
-            w1_bf[:].rearrange("p (t m j) -> p m j t", t=PACK, j=PACK),
-            w1_raw[:].rearrange("p j (m t) -> p m j t", t=PACK),
-        )
-        wo_raw = sbt("wo_raw", [P, PACK, R], F32, "w_raw")
-        nc.sync.dma_start(wo_raw[:], wo.rearrange("(p j) r -> p j r", j=PACK))
-        w1_codes = sbt("w1_codes", [P, R], U32)
-        w1_scales = sbt("w1_scales", [P, R], U8)
-        nc.vector.quantize_mx(out=w1_codes[:].bitcast(FP8X4), scales=w1_scales[:], in_=w1_bf[:])
+        w1_bf = [sbt("w1_bf%d" % u, [P, PACK * R // 2], BF16) for u in range(2)]
+        w1_codes = [sbt("w1_codes%d" % u, [P, R // 2], U32) for u in range(2)]
+        w1_scales = [sbt("w1_scales%d" % u, [P, R // 2], U8) for u in range(2)]
+        w1_dealt = w1_raw[:].rearrange("p j (m t) -> p m j t", t=PACK)
+        nc.vector.tensor_copy(w1_bf[0][:].rearrange("p (t m j) -> p m j t", t=2, j=PACK), w1_dealt[:, :, :, 0:2])
+        nc.scalar.copy(w1_bf[1][:].rearrange("p (t m j) -> p m j t", t=2, j=PACK), w1_dealt[:, :, :, 2:4])
+        nc.vector.quantize_mx(out=w1_codes[0][:].bitcast(FP8X4), scales=w1_scales[0][:], in_=w1_bf[0][:])
         gw = sbt("gw", [P, J], U32)
         nc.vector.tensor_copy(gw[:], tabw[:].indirect(slot_list[:]))
-        old_sb = sbt("old_sb", [P, PACK, J], F32, "tabw_old")
-        nc.sync.dma_start(old_sb[:], old.rearrange("(p t) j -> p t j", t=PACK))
+        nc.vector.quantize_mx(out=w1_codes[1][:].bitcast(FP8X4), scales=w1_scales[1][:], in_=w1_bf[1][:])
 
-        a_banks = [ps.tile([P, J], F32, name="a%d" % t) for t in range(PACK)]
-        for t in range(PACK):
-            cols = slice(t * P, (t + 1) * P)
+        a_banks = {}
+
+        def first_product(t, tag):
+            a_banks[t] = ps.tile([P, J], F32, name="a%d" % t, tag=tag)
+            cols = slice(t % 2 * P, (t % 2 + 1) * P)
             nc.tensor.matmul_mx(
-                out=a_banks[t][:], lhsT=w1_codes[:, cols].bitcast(FP8X4), lhsT_scale=w1_scales[:, cols],
+                out=a_banks[t][:], lhsT=w1_codes[t // 2][:, cols].bitcast(FP8X4), lhsT_scale=w1_scales[t // 2][:, cols],
                 rhs=gw[:].bitcast(FP8X4), rhs_scale=gs[:], start=True, stop=True,
             )
+
+        for t in range(3):
+            first_product(t, "a%d" % t)
 
         dy_bf = sbt("dy_bf", [P, PACK * M], BF16)
         nc.vector.tensor_copy(
@@ -103,11 +113,7 @@ def tile_attend_cpickact_pl_kernel(tc, tab_words, tab_scales, w1, bias, gain, pw
 
         h1 = [sbt("h1_%d" % t, [P, J], F32) for t in range(PACK)]
         h2 = [sbt("h2_%d" % t, [P, J], F32) for t in range(PACK)]
-        sq = [sbt("sq_%d" % t, [P, J], F32) for t in range(PACK)]
-        s = [sbt("s_%d" % t, [P, M], F32) for t in range(PACK)]
-        nsil = [sbt("nsil_%d" % t, [P, M], F32) for t in range(PACK)]
-        th = [sbt("th_%d" % t, [P, M], F32) for t in range(PACK)]
-        nsig = [sbt("nsig_%d" % t, [P, M], F32) for t in range(PACK)]
+        sq, s, nsil, nsig = {}, {}, {}, {}
         part = [sbt("part_%d" % t, [P, M], F32) for t in range(PACK)]
         nda = [sbt("nda_%d" % t, [P, J], F32) for t in range(PACK)]
         y = sbt("y", [P, PACK, J], F32)
@@ -117,28 +123,43 @@ def tile_attend_cpickact_pl_kernel(tc, tab_words, tab_scales, w1, bias, gain, pw
             nc.scalar.activation(h2[t][:], h1[t][:], ACT.Copy, scale=gain_sb[:, t : t + 1])
 
         def pick(t):
-            nc.vector.tensor_tensor(s[t][:], h2[t][:].indirect(pick_lists[:]), pw_row[:], ALU.mult)
+            nc.vector.tensor_tensor(s[t], h2[t][:].indirect(pick_lists[:]), pw_row[:], ALU.mult)
 
-        def silu_parts(t):
-            nc.scalar.activation(nsil[t][:], s[t][:], ACT.Silu, scale=-1.0)
-            nc.scalar.activation(th[t][:], s[t][:], ACT.Tanh, scale=0.5)
-            nc.scalar.activation(nsig[t][:], th[t][:], ACT.Copy, scale=-0.5, bias=-0.5)
+        def silu_parts(t, nsil_tag, th_tag):
+            nsil[t] = sbt("nsil_%d" % t, [P, M], F32, nsil_tag)
+            th = sbt("th_%d" % t, [P, M], F32, th_tag)
+            nsig[t] = sbt("nsig_%d" % t, [P, M], F32)
+            nc.scalar.activation(nsil[t][:], s[t], ACT.Silu, scale=-1.0)
+            nc.scalar.activation(th[:], s[t], ACT.Tanh, scale=0.5)
+            nc.scalar.activation(nsig[t][:], th[:], ACT.Copy, scale=-0.5, bias=-0.5)
 
-        forward(0)
-        pick(0)
-        forward(1)
+        def square(t, tag):
+            sq[t] = sbt("sq_%d" % t, [P, J], F32, tag)
+            nc.scalar.activation(sq[t][:], h1[t][:], ACT.Square)
 
-        wo_bf = sbt("wo_bf", [P, PACK * R], BF16)
-        nc.vector.tensor_copy(
-            wo_bf[:].rearrange("p (c i j) -> p c j i", i=4, j=PACK),
-            wo_raw[:].rearrange("p j (c i) -> p c j i", i=4),
-        )
-        pick(1)
+        wo_bf = [sbt("wo_bf%d" % u, [P, PACK * R // 2], BF16) for u in range(2)]
         wo_codes = sbt("wo_codes", [P, R], U32)
         wo_scales = sbt("wo_scales", [P, R], U8)
-        nc.vector.quantize_mx(out=wo_codes[:].bitcast(FP8X4), scales=wo_scales[:], in_=wo_bf[:])
-        forward(2)
-        forward(3)
+
+        def wo_round(u):
+            nc.vector.tensor_copy(
+                wo_bf[u][:].rearrange("p (c i j) -> p c j i", i=4, j=PACK),
+                wo_raw[u][:].rearrange("p j (c i) -> p c j i", i=4),
+            )
+
+        def wo_quantize(u):
+            cols = slice(u * R // 2, (u + 1) * R // 2)
+            nc.vector.quantize_mx(out=wo_codes[:, cols].bitcast(FP8X4), scales=wo_scales[:, cols], in_=wo_bf[u][:])
+
+        wo_round(0)
+        wo_round(1)
+        wo_quantize(0)
+        wo_quantize(1)
+        s_first = sbt("s_first", [P, 3, M], F32, "wo_bf1")
+        for t in range(3):
+            s[t] = s_first[:, t, :]
+            forward(t)
+            pick(t)
         c0t_banks = [ps.tile([P, R], F32, name="c0t_bank%d" % h, tag="c0t%d" % h) for h in range(2)]
         cpt = [sbt("cpt_%d" % h, [P, PACK, P], F32) for h in range(2)]
         for h in range(2):
@@ -147,24 +168,22 @@ def tile_attend_cpickact_pl_kernel(tc, tab_words, tab_scales, w1, bias, gain, pw
                 out=c0t_banks[h][:], lhsT=dy_codes[:, cols].bitcast(FP8X4), lhsT_scale=dy_scales[:, cols],
                 rhs=wo_codes[:].bitcast(FP8X4), rhs_scale=wo_scales[:], start=True, stop=True,
             )
-        pick(2)
-        silu_parts(0)
         for h in range(2):
             nc.scalar.activation(
                 cpt[h][:], c0t_banks[h][:].rearrange("m (p t) -> m t p", t=PACK), ACT.Copy, scale=pw_cols[:, h : h + 1]
             )
+        silu_parts(0, "dy_codes", "wo_codes")
         cp_banks = [ps.tile([P, 2, 2, P], F32, name="cp_bank%d" % u) for u in range(2)]
         for t in range(PACK):
             for h in range(2):
                 nc.tensor.transpose(cp_banks[t // 2][:, t % 2, h, :], cpt[h][:, t, :], ident[:])
-        pick(3)
-        silu_parts(1)
-        nc.scalar.activation(sq[0][:], h1[0][:], ACT.Square)
-        silu_parts(2)
-        nc.scalar.activation(sq[1][:], h1[1][:], ACT.Square)
-        silu_parts(3)
-        nc.scalar.activation(sq[2][:], h1[2][:], ACT.Square)
-        nc.scalar.activation(sq[3][:], h1[3][:], ACT.Square)
+        first_product(3, "c0t1")
+        silu_parts(1, "dy_scales", "wo_codes")
+        forward(3)
+        s_last = sbt("s_last", [P, M], F32)
+        s[3] = s_last[:]
+        square(0, "cpt_0")
+        square(1, "cpt_1")
 
         def grad_part(t):
             nc.vector.scalar_tensor_tensor(
@@ -192,7 +211,12 @@ def tile_attend_cpickact_pl_kernel(tc, tab_words, tab_scales, w1, bias, gain, pw
         grad_part(0)
         grad_part(1)
         scatter(0)
+        pick(3)
+        silu_parts(2, "wo_scales", "wo_codes")
         scatter(1)
+        silu_parts(3, None, "wo_codes")
+        square(2, "h2_3")
+        square(3, "nsig_1")
         tanh_grad(0, whole)
         grad_part(2)
         add_old(0, whole)

@@ -63,8 +63,8 @@ def tile_attend_cpickact_pl_kernel(tc, tab_words, tab_scales, w1, bias, gain, pw
         for t in range(PACK):
             nc.vector.memset(s1[t][:], 0.0)
 
-        warm = sbt("warm", [P, 8], F32)
-        nc.scalar.activation(warm[:], s1[0][:, 0:8], ACT.Silu)
+        zero = sbt("zero", [P, 1], F32)
+        nc.scalar.activation(zero[:], s1[0][:, 0:1], ACT.Silu)
 
         pw_bank = ps.tile([P, 2, P], F32, name="pw_bank", tag="c0t0")
         for h in range(2):
@@ -112,7 +112,7 @@ def tile_attend_cpickact_pl_kernel(tc, tab_words, tab_scales, w1, bias, gain, pw
         nc.vector.quantize_mx(out=dy_codes[:].bitcast(FP8X4), scales=dy_scales[:], in_=dy_bf[:])
 
         h1 = [sbt("h1_%d" % t, [P, J], F32) for t in range(PACK)]
-        h2 = [sbt("h2_%d" % t, [P, J], F32) for t in range(PACK)]
+        h2 = {}
         sq, s, nsil, nsig = {}, {}, {}, {}
         part = [sbt("part_%d" % t, [P, M], F32) for t in range(PACK)]
         nda = [sbt("nda_%d" % t, [P, J], F32) for t in range(PACK)]
@@ -120,7 +120,12 @@ def tile_attend_cpickact_pl_kernel(tc, tab_words, tab_scales, w1, bias, gain, pw
 
         def forward(t):
             nc.scalar.activation(h1[t][:], a_banks[t][:], ACT.Tanh, bias=bias_sb[:, t : t + 1])
-            nc.scalar.activation(h2[t][:], h1[t][:], ACT.Copy, scale=gain_sb[:, t : t + 1])
+            if t == 2:
+                h2[t] = sbt("h2_2", [P, J], F32, "h2_0")
+                nc.vector.tensor_scalar(h2[t][:], h1[t][:], gain_sb[:, t : t + 1], None, ALU.mult)
+            else:
+                h2[t] = sbt("h2_%d" % t, [P, J], F32)
+                nc.scalar.activation(h2[t][:], h1[t][:], ACT.Copy, scale=gain_sb[:, t : t + 1])
 
         def pick(t):
             nc.vector.tensor_tensor(s[t], h2[t][:].indirect(pick_lists[:]), pw_row[:], ALU.mult)
@@ -129,8 +134,8 @@ def tile_attend_cpickact_pl_kernel(tc, tab_words, tab_scales, w1, bias, gain, pw
             nsil[t] = sbt("nsil_%d" % t, [P, M], F32, nsil_tag)
             th = sbt("th_%d" % t, [P, M], F32, th_tag)
             nsig[t] = sbt("nsig_%d" % t, [P, M], F32)
-            nc.scalar.activation(nsil[t][:], s[t], ACT.Silu, scale=-1.0)
-            nc.scalar.activation(th[:], s[t], ACT.Tanh, scale=0.5)
+            nc.scalar.activation(nsil[t][:], s[t], ACT.Silu, scale=-1.0, bias=zero[:])
+            nc.scalar.activation(th[:], s[t], ACT.Tanh, scale=0.5, bias=zero[:])
             nc.scalar.activation(nsig[t][:], th[:], ACT.Copy, scale=-0.5, bias=-0.5)
 
         def square(t, tag):
@@ -153,21 +158,22 @@ def tile_attend_cpickact_pl_kernel(tc, tab_words, tab_scales, w1, bias, gain, pw
 
         wo_round(0)
         wo_round(1)
-        wo_quantize(0)
-        wo_quantize(1)
+        c0t_banks = [ps.tile([P, R], F32, name="c0t_bank%d" % h, tag="c0t%d" % h) for h in range(2)]
+        for u in range(2):
+            wo_quantize(u)
+            r_cols = slice(u * R // 2, (u + 1) * R // 2)
+            for h in range(2):
+                m_cols = slice(h * P, (h + 1) * P)
+                nc.tensor.matmul_mx(
+                    out=c0t_banks[h][:, r_cols], lhsT=dy_codes[:, m_cols].bitcast(FP8X4), lhsT_scale=dy_scales[:, m_cols],
+                    rhs=wo_codes[:, r_cols].bitcast(FP8X4), rhs_scale=wo_scales[:, r_cols], start=True, stop=True,
+                )
         s_first = sbt("s_first", [P, 3, M], F32, "wo_bf1")
         for t in range(3):
             s[t] = s_first[:, t, :]
             forward(t)
             pick(t)
-        c0t_banks = [ps.tile([P, R], F32, name="c0t_bank%d" % h, tag="c0t%d" % h) for h in range(2)]
         cpt = [sbt("cpt_%d" % h, [P, PACK, P], F32) for h in range(2)]
-        for h in range(2):
-            cols = slice(h * P, (h + 1) * P)
-            nc.tensor.matmul_mx(
-                out=c0t_banks[h][:], lhsT=dy_codes[:, cols].bitcast(FP8X4), lhsT_scale=dy_scales[:, cols],
-                rhs=wo_codes[:].bitcast(FP8X4), rhs_scale=wo_scales[:], start=True, stop=True,
-            )
         for h in range(2):
             nc.scalar.activation(
                 cpt[h][:], c0t_banks[h][:].rearrange("m (p t) -> m t p", t=PACK), ACT.Copy, scale=pw_cols[:, h : h + 1]
@@ -182,8 +188,6 @@ def tile_attend_cpickact_pl_kernel(tc, tab_words, tab_scales, w1, bias, gain, pw
         forward(3)
         s_last = sbt("s_last", [P, M], F32)
         s[3] = s_last[:]
-        square(0, "cpt_0")
-        square(1, "cpt_1")
 
         def grad_part(t):
             nc.vector.scalar_tensor_tensor(
@@ -207,31 +211,65 @@ def tile_attend_cpickact_pl_kernel(tc, tab_words, tab_scales, w1, bias, gain, pw
                 y[:, t, cols], nda[t][:, cols], neg_gain[:, t : t + 1], old_sb[:, t, cols], ALU.mult, ALU.add
             )
 
+        slope, da, turned = {}, {}, {}
+
+        def tanh_slope(t):
+            square(t, "cpt_%d" % t)
+            slope[t] = sbt("slope_%d" % t, [P, J], F32, "h1_%d" % t)
+            nc.scalar.activation(
+                slope[t][:], sq[t][:], ACT.Identity, scale=neg_gain[:, t : t + 1], bias=gain_sb[:, t : t + 1]
+            )
+
+        def times_slope(t):
+            nc.vector.tensor_tensor(nda[t][:], s1[t][:], slope[t][:], ALU.mult)
+
+        def add_old_turned(t):
+            bank = ps.tile([P, J], F32, name="yt_bank%d" % t, tag=("c0t1", "cp_bank0")[t])
+            blocks = [slice(c * P, (c + 1) * P) for c in range(J // P)]
+            for cols in blocks:
+                nc.tensor.matmul(
+                    bank[:, cols], lhsT=old_sb[:, t, cols], rhs=ident[:], is_transpose=True, start=cols == blocks[0], stop=False
+                )
+            for cols in blocks:
+                nc.tensor.matmul(
+                    bank[:, cols], lhsT=nda[t][:, cols], rhs=ident[:], is_transpose=True, start=False, stop=cols == blocks[-1]
+                )
+            turned[t] = sbt("yt_%d" % t, [P, J], F32)
+            nc.scalar.copy(turned[t][:], bank[:])
+
+        def turn_back(t):
+            bank = ps.tile([P, J], F32, name="y_bank%d" % t, tag="a%d" % t)
+            for c in range(J // P):
+                cols = slice(c * P, (c + 1) * P)
+                nc.tensor.transpose(bank[:, cols], turned[t][:, cols], ident[:])
+            nc.scalar.copy(y[:, t, :], bank[:])
+            nc.sync.dma_start(out_rows[:, t, :], y[:, t, :])
+
         whole = slice(0, J)
         grad_part(0)
-        grad_part(1)
         scatter(0)
-        pick(3)
-        silu_parts(2, "wo_scales", "wo_codes")
+        grad_part(1)
         scatter(1)
-        silu_parts(3, None, "wo_codes")
-        square(2, "h2_3")
-        square(3, "nsig_1")
-        tanh_grad(0, whole)
+        pick(3)
+        for t in range(2):
+            tanh_slope(t)
+            times_slope(t)
+        silu_parts(2, "wo_scales", "wo_codes")
         grad_part(2)
-        add_old(0, whole)
-        nc.sync.dma_start(out_rows[:, 0, :], y[:, 0, :])
-        tanh_grad(1, whole)
         scatter(2)
-        add_old(1, whole)
-        nc.sync.dma_start(out_rows[:, 1, :], y[:, 1, :])
+        silu_parts(3, None, "wo_codes")
         grad_part(3)
-        tanh_grad(2, whole)
         scatter(3)
+        for t in range(2):
+            square(2 + t, ("h2_3", "nsig_1")[t])
+            add_old_turned(t)
+        for t in range(2):
+            turn_back(t)
+        halves = [slice(0, J // 2), slice(J // 2, J)]
+        tanh_grad(2, whole)
+        tanh_grad(3, halves[0])
         add_old(2, whole)
         nc.sync.dma_start(out_rows[:, 2, :], y[:, 2, :])
-        halves = [slice(0, J // 2), slice(J // 2, J)]
-        tanh_grad(3, halves[0])
         tanh_grad(3, halves[1])
         add_old(3, halves[0])
         add_old(3, halves[1])
@@ -249,8 +287,9 @@ def tile_attend_cpickact_pl_kernel(tc, tab_words, tab_scales, w1, bias, gain, pw
             y[:, :, halves[1]].rearrange("p t (c i) -> p c t i", i=4),
         )
         words_out = out_1[0].rearrange("p n t -> p (n t)").bitcast(I32)
-        for u in (1, 0):
+        for u in range(2):
             nc.vector.quantize_mx(out=y_codes[:, halves[u]].bitcast(FP8X4), scales=y_scales[:, halves[u]], in_=y_bf[u][:])
             nc.sync.dma_start(words_out[:, halves[u]], y_codes[:, halves[u]].bitcast(I32))
         for q in range(4):
-            nc.scalar.dma_start(out_2[0, 4 * q : 4 * q + 4, :].bitcast(I32), y_scales[32 * q : 32 * q + 4, :].bitcast(I32))
+            queue = nc.sync if q == 0 else nc.scalar
+            queue.dma_start(out_2[0, 4 * q : 4 * q + 4, :].bitcast(I32), y_scales[32 * q : 32 * q + 4, :].bitcast(I32))

from contextlib import ExitStack

import concourse.mybir as mybir
from concourse.masks import make_identity

K, R, F, T, J, M = 512, 512, 512, 2048, 512, 256
FLOPS = 2 * K * R * J + 2 * F * R * M

F32 = mybir.dt.float32
BF16 = mybir.dt.bfloat16
I32 = mybir.dt.int32
U32 = mybir.dt.uint32
U16 = mybir.dt.uint16
U8 = mybir.dt.uint8
FP8X4 = mybir.dt.float8_e4m3fn_x4
ACT = mybir.ActivationFunctionType
ALU = mybir.AluOpType

P = 128
PACK = 4


def tile_attend_cpickact_pl_kernel(tc, tab_words, tab_scales, w1, bias, gain, pw, wo, dy, old, offs, offs2, out_0, out_1, out_2):
    nc = tc.nc
    with ExitStack() as ctx:
        sb = ctx.enter_context(tc.tile_pool(name="sb", bufs=1))
        ps = ctx.enter_context(tc.psum_pool(name="ps", bufs=1))

        def sbt(name, shape, dtype, tag=None):
            return sb.tile(shape, dtype, name=name, tag=tag or name, align_bytes=64)

        slot_list = sbt("slot_list", [P, J // 16], U16)
        pick_lists = sbt("pick_lists", [P, M // 16], U16)
        tabw = sbt("tabw", [P, T], U32)
        tabs = sbt("tabs", [P, T], U8)
        w1_raw = sbt("w1_raw", [P, PACK, R], F32)
        wo_raw = [sbt("wo_raw%d" % u, [P, PACK, R // 2], F32) for u in range(2)]
        tabs_in = sbt("tabs_in", [P, T // 4], I32)
        dy_raw = sbt("dy_raw", [P, PACK, M], F32)
        old_sb = sbt("old_sb", [P, PACK, J], F32)
        bias_sb = sbt("bias_sb", [P, PACK], F32)
        gain_sb = sbt("gain_sb", [P, PACK], F32)
        pw_cols = sbt("pw_cols", [P, 2], F32)
        s1 = [sbt("s1_%d" % t, [P, J], F32) for t in range(PACK)]

        for q in range(4):
            queue = nc.sync if q % 2 == 0 else nc.scalar
            queue.dma_start(tabs_in[32 * q : 32 * q + 4, :], tab_scales[0, 4 * q : 4 * q + 4, :].bitcast(I32))
        nc.vector.memset(tabs[:].bitcast(I32), 0)
        nc.sync.dma_start(slot_list[:], offs)
        nc.scalar.dma_start(pw_cols[:], pw.rearrange("o (p h) -> p (o h)", h=2))
        nc.sync.dma_start(w1_raw[:], w1.rearrange("(p j) r -> p j r", j=PACK))
        nc.sync.dma_start(tabw[:].bitcast(I32), tab_words[0].rearrange("p n t -> p (n t)").bitcast(I32))
        nc.sync.dma_start(bias_sb[:], bias.rearrange("(p t) o -> p (t o)", t=PACK))
        nc.sync.dma_start(gain_sb[:], gain.rearrange("(p t) o -> p (t o)", t=PACK))
        nc.sync.dma_start(pick_lists[:], offs2)
        nc.sync.dma_start(dy_raw[:], dy.rearrange("(p j) m -> p j m", j=PACK))
        for u in range(2):
            nc.sync.dma_start(wo_raw[u][:], wo.rearrange("(p j) r -> p j r", j=PACK)[:, :, u * R // 2 : (u + 1) * R // 2])
        nc.sync.dma_start(old_sb[:], old.rearrange("(p t) j -> p t j", t=PACK))
        ident = sbt("ident", [P, P], F32)
        make_identity(nc, ident[:])
        for t in range(PACK):
            nc.vector.memset(s1[t][:], 0.0)

        zero = sbt("zero", [P, 1], F32)
        nc.scalar.activation(zero[:], s1[0][:, 0:1], ACT.Silu)

        pw_bank = ps.tile([P, 2, P], F32, name="pw_bank", tag="c0t0")
        for h in range(2):
            nc.tensor.transpose(pw_bank[:, h, :], pw_cols[:, h : h + 1].to_broadcast([P, P]), ident[:])
        pw_row = sbt("pw_row", [P, M], F32)
        nc.scalar.copy(pw_row[:].rearrange("q (p h) -> q p h", h=2), pw_bank[:].rearrange("q h p -> q p h"))
        neg_gain = sbt("neg_gain", [P, PACK], F32)
        nc.scalar.activation(neg_gain[:], gain_sb[:], ACT.Copy, scale=-1.0)

        for q in range(4):
            nc.vector.tensor_copy(tabs[32 * q : 32 * q + 4, :].bitcast(I32), tabs_in[32 * q : 32 * q + 4, :])
        gs = sbt("gs", [P, J], U8)
        nc.vector.tensor_copy(gs[:], tabs[:].indirect(slot_list[:]))
        w1_bf = [sbt("w1_bf%d" % u, [P, PACK * R // 2], BF16) for u in range(2)]
        w1_codes = [sbt("w1_codes%d" % u, [P, R // 2], U32) for u in range(2)]
        w1_scales = [sbt("w1_scales%d" % u, [P, R // 2], U8) for u in range(2)]
        w1_dealt = w1_raw[:].rearrange("p j (m t) -> p m j t", t=PACK)
        nc.vector.tensor_copy(w1_bf[0][:].rearrange("p (t m j) -> p m j t", t=2, j=PACK), w1_dealt[:, :, :, 0:2])
        nc.scalar.copy(w1_bf[1][:].rearrange("p (t m j) -> p m j t", t=2, j=PACK), w1_dealt[:, :, :, 2:4])
        nc.vector.quantize_mx(out=w1_codes[0][:].bitcast(FP8X4), scales=w1_scales[0][:], in_=w1_bf[0][:])
        gw = sbt("gw", [P, J], U32)
        nc.vector.tensor_copy(gw[:], tabw[:].indirect(slot_list[:]))
        nc.vector.quantize_mx(out=w1_codes[1][:].bitcast(FP8X4), scales=w1_scales[1][:], in_=w1_bf[1][:])

        a_banks = {}

        def first_product(t, tag):
            a_banks[t] = ps.tile([P, J], F32, name="a%d" % t, tag=tag)
            cols = slice(t % 2 * P, (t % 2 + 1) * P)
            nc.tensor.matmul_mx(
                out=a_banks[t][:], lhsT=w1_codes[t // 2][:, cols].bitcast(FP8X4), lhsT_scale=w1_scales[t // 2][:, cols],
                rhs=gw[:].bitcast(FP8X4), rhs_scale=gs[:], start=True, stop=True,
            )

        for t in range(3):
            first_product(t, "a%d" % t)

        dy_bf = sbt("dy_bf", [P, PACK * M], BF16)
        nc.vector.tensor_copy(
            dy_bf[:].rearrange("p (h n j) -> p n j h", h=2, j=PACK),
            dy_raw[:].rearrange("p j (n h) -> p n j h", h=2),
        )
        dy_codes = sbt("dy_codes", [P, M], U32)
        dy_scales = sbt("dy_scales", [P, M], U8)
        nc.vector.quantize_mx(out=dy_codes[:].bitcast(FP8X4), scales=dy_scales[:], in_=dy_bf[:])

        h1 = [sbt("h1_%d" % t, [P, J], F32) for t in range(PACK)]
        h2 = {}
        sq, s, nsil, nsig = {}, {}, {}, {}
        part = [sbt("part_%d" % t, [P, M], F32) for t in range(PACK)]
        nda = [sbt("nda_%d" % t, [P, J], F32) for t in range(PACK)]
        y = sbt("y", [P, PACK, J], F32)

        def forward(t):
            nc.scalar.activation(h1[t][:], a_banks[t][:], ACT.Tanh, bias=bias_sb[:, t : t + 1])
            if t == 2:
                h2[t] = sbt("h2_2", [P, J], F32, "h2_0")
                nc.vector.tensor_scalar(h2[t][:], h1[t][:], gain_sb[:, t : t + 1], None, ALU.mult)
            else:
                h2[t] = sbt("h2_%d" % t, [P, J], F32)
                nc.scalar.activation(h2[t][:], h1[t][:], ACT.Copy, scale=gain_sb[:, t : t + 1])

        def pick(t):
            nc.vector.tensor_tensor(s[t], h2[t][:].indirect(pick_lists[:]), pw_row[:], ALU.mult)

        def silu_parts(t, nsil_tag, th_tag):
            nsil[t] = sbt("nsil_%d" % t, [P, M], F32, nsil_tag)
            th = sbt("th_%d" % t, [P, M], F32, th_tag)
            nsig[t] = sbt("nsig_%d" % t, [P, M], F32)
            nc.scalar.activation(nsil[t][:], s[t], ACT.Silu, scale=-1.0, bias=zero[:])
            nc.scalar.activation(th[:], s[t], ACT.Tanh, scale=0.5, bias=zero[:])
            nc.scalar.activation(nsig[t][:], th[:], ACT.Copy, scale=-0.5, bias=-0.5)

        def square(t, tag):
            sq[t] = sbt("sq_%d" % t, [P, J], F32, tag)
            nc.scalar.activation(sq[t][:], h1[t][:], ACT.Square)

        wo_bf = [sbt("wo_bf%d" % u, [P, PACK * R // 2], BF16) for u in range(2)]
        wo_codes = sbt("wo_codes", [P, R], U32)
        wo_scales = sbt("wo_scales", [P, R], U8)

        def wo_round(u):
            nc.vector.tensor_copy(
                wo_bf[u][:].rearrange("p (c i j) -> p c j i", i=4, j=PACK),
                wo_raw[u][:].rearrange("p j (c i) -> p c j i", i=4),
            )

        def wo_quantize(u):
            cols = slice(u * R // 2, (u + 1) * R // 2)
            nc.vector.quantize_mx(out=wo_codes[:, cols].bitcast(FP8X4), scales=wo_scales[:, cols], in_=wo_bf[u][:])

        wo_round(0)
        wo_round(1)
        c0t_banks = [ps.tile([P, R], F32, name="c0t_bank%d" % h, tag="c0t%d" % h) for h in range(2)]
        for u in range(2):
            wo_quantize(u)
            r_cols = slice(u * R // 2, (u + 1) * R // 2)
            for h in range(2):
                m_cols = slice(h * P, (h + 1) * P)
                nc.tensor.matmul_mx(
                    out=c0t_banks[h][:, r_cols], lhsT=dy_codes[:, m_cols].bitcast(FP8X4), lhsT_scale=dy_scales[:, m_cols],
                    rhs=wo_codes[:, r_cols].bitcast(FP8X4), rhs_scale=wo_scales[:, r_cols], start=True, stop=True,
                )
        s_first = sbt("s_first", [P, 3, M], F32, "wo_bf1")
        for t in range(3):
            s[t] = s_first[:, t, :]
            forward(t)
            pick(t)
        cpt = [sbt("cpt_%d" % h, [P, PACK, P], F32) for h in range(2)]
        for h in range(2):
            nc.scalar.activation(
                cpt[h][:], c0t_banks[h][:].rearrange("m (p t) -> m t p", t=PACK), ACT.Copy, scale=pw_cols[:, h : h + 1]
            )
        silu_parts(0, "dy_codes", "wo_codes")
        cp_banks = [ps.tile([P, 2, 2, P], F32, name="cp_bank%d" % u) for u in range(2)]
        for t in range(PACK):
            for h in range(2):
                nc.tensor.transpose(cp_banks[t // 2][:, t % 2, h, :], cpt[h][:, t, :], ident[:])
        first_product(3, "c0t1")
        silu_parts(1, "dy_scales", "wo_codes")
        forward(3)
        s_last = sbt("s_last", [P, M], F32)
        s[3] = s_last[:]

        def grad_part(t):
            nc.vector.scalar_tensor_tensor(
                part[t][:].rearrange("r (n h) -> r n h", h=2),
                nsil[t][:].rearrange("r (n h) -> r n h", h=2),
                1.0,
                cp_banks[t // 2][:, t % 2, :, :].rearrange("r h n -> r n h"),
                ALU.subtract, ALU.mult,
            )

        def scatter(t):
            nc.vector.tensor_tensor(s1[t][:].indirect(pick_lists[:]), part[t][:], nsig[t][:], ALU.mult)

        def tanh_grad(t, cols):
            nc.vector.scalar_tensor_tensor(nda[t][:, cols], sq[t][:, cols], 1.0, s1[t][:, cols], ALU.subtract, ALU.mult)

        out_rows = out_0.rearrange("(p t) j -> p t j", t=PACK)

        def add_old(t, cols):
            nc.vector.scalar_tensor_tensor(
                y[:, t, cols], nda[t][:, cols], neg_gain[:, t : t + 1], old_sb[:, t, cols], ALU.mult, ALU.add
            )

        slope, da, turned = {}, {}, {}

        def tanh_slope(t):
            square(t, "cpt_%d" % t)
            slope[t] = sbt("slope_%d" % t, [P, J], F32, "h1_%d" % t)
            nc.scalar.activation(
                slope[t][:], sq[t][:], ACT.Identity, scale=neg_gain[:, t : t + 1], bias=gain_sb[:, t : t + 1]
            )

        def times_slope(t):
            nc.vector.tensor_tensor(nda[t][:], s1[t][:], slope[t][:], ALU.mult)

        def add_old_turned(t):
            bank = ps.tile([P, J], F32, name="yt_bank%d" % t, tag=("c0t1", "cp_bank0")[t])
            blocks = [slice(c * P, (c + 1) * P) for c in range(J // P)]
            for cols in blocks:
                nc.tensor.matmul(
                    bank[:, cols], lhsT=old_sb[:, t, cols], rhs=ident[:], is_transpose=True, start=cols == blocks[0], stop=False
                )
            for cols in blocks:
                nc.tensor.matmul(
                    bank[:, cols], lhsT=nda[t][:, cols], rhs=ident[:], is_transpose=True, start=False, stop=cols == blocks[-1]
                )
            turned[t] = sbt("yt_%d" % t, [P, J], F32)
            nc.scalar.copy(turned[t][:], bank[:])

        def turn_back(t):
            bank = ps.tile([P, J], F32, name="y_bank%d" % t, tag="a%d" % t)
            for c in range(J // P):
                cols = slice(c * P, (c + 1) * P)
                nc.tensor.transpose(bank[:, cols], turned[t][:, cols], ident[:])
            nc.scalar.copy(y[:, t, :], bank[:])
            nc.sync.dma_start(out_rows[:, t, :], y[:, t, :])

        whole = slice(0, J)
        grad_part(0)
        scatter(0)
        grad_part(1)
        scatter(1)
        pick(3)
        for t in range(2):
            tanh_slope(t)
            times_slope(t)
        silu_parts(2, "wo_scales", "wo_codes")
        grad_part(2)
        scatter(2)
        silu_parts(3, None, "wo_codes")
        grad_part(3)
        scatter(3)
        for t in range(2):
            square(2 + t, ("h2_3", "nsig_1")[t])
            add_old_turned(t)
        for t in range(2):
            turn_back(t)
        halves = [slice(0, J // 2), slice(J // 2, J)]
        tanh_grad(2, whole)
        tanh_grad(3, halves[0])
        add_old(2, whole)
        nc.sync.dma_start(out_rows[:, 2, :], y[:, 2, :])
        tanh_grad(3, halves[1])
        add_old(3, halves[0])
        add_old(3, halves[1])
        nc.sync.dma_start(out_rows[:, 3, :], y[:, 3, :])

        y_bf = [sbt("y_bf%d" % u, [P, PACK * J // 2], BF16) for u in range(2)]
        y_codes = sbt("y_codes", [P, J], U32)
        y_scales = sbt("y_scales", [P, J], U8)
        nc.scalar.copy(
            y_bf[0][:].rearrange("p (c i t) -> p c t i", i=4, t=PACK),
            y[:, :, halves[0]].rearrange("p t (c i) -> p c t i", i=4),
        )
        nc.vector.tensor_copy(
            y_bf[1][:].rearrange("p (c i t) -> p c t i", i=4, t=PACK),
            y[:, :, halves[1]].rearrange("p t (c i) -> p c t i", i=4),
        )
        words_out = out_1[0].rearrange("p n t -> p (n t)").bitcast(I32)
        for u in range(2):
            nc.vector.quantize_mx(out=y_codes[:, halves[u]].bitcast(FP8X4), scales=y_scales[:, halves[u]], in_=y_bf[u][:])
            nc.sync.dma_start(words_out[:, halves[u]], y_codes[:, halves[u]].bitcast(I32))
        for q in range(4):
            queue = nc.sync if q == 0 else nc.scalar
            queue.dma_start(out_2[0, 4 * q : 4 * q + 4, :].bitcast(I32), y_scales[32 * q : 32 * q + 4, :].bitcast(I32))
